import numpy as np
import ml_dtypes


def mxq(x, axis, fmt="e4m3"):
    dtype, down = {"e4m3": (ml_dtypes.float8_e4m3fn, 7), "e5m2": (ml_dtypes.float8_e5m2, 14)}[fmt]
    v = np.moveaxis(np.asarray(x, np.float32).astype(ml_dtypes.bfloat16).astype(np.float64), axis, -1)
    blocks = v.reshape(v.shape[:-1] + (-1, 32))
    amax = np.abs(blocks).max(-1, keepdims=True)
    byte = np.maximum(np.where(amax > 0, np.frexp(amax)[1] - 1 + 127, 0) - down, 1)
    scale = np.exp2(byte - 127.0)
    codes = (blocks / scale).astype(np.float32).astype(dtype).astype(np.float64)
    return np.moveaxis((codes * scale).reshape(v.shape), -1, axis)


WIDE = False


def mx_kscale(k):
    if not WIDE:
        return np.ones(k)
    levels = np.array([10, -10, 5, -5, 0])
    if k % 512:
        return np.exp2(np.random.permutation(np.resize(levels, k // 32))).repeat(32)
    a = np.empty((k // 512, 16))
    for p in range(k // 512):
        a[p, :8] = np.random.permutation(np.resize(levels, 8))
        for g in range(8):
            far = levels[np.abs(levels - a[p, g]) >= 10]
            a[p, g + 8] = far[np.random.randint(len(far))]
    return np.exp2(a.ravel()).repeat(32)


BF16 = ml_dtypes.bfloat16


def bf(x):
    return np.asarray(x, np.float32).astype(BF16)


def f64(x):
    return np.asarray(x).astype(np.float64)


E2M1 = np.array([0.0, 0.5, 1.0, 1.5, 2.0, 3.0, 4.0, 6.0, -0.0, -0.5, -1.0, -1.5, -2.0, -3.0, -4.0, -6.0])


def pack_weight(w, fmt):
    k, n = w.shape
    w = f64(bf(w)).reshape(k // 32, 32, n)
    amax = np.abs(w).max(1)
    if fmt == "e4m3":
        byte = np.frexp(amax)[1] - 1 + 127 - 7
    else:
        mant, ex = np.frexp(amax / 6.0)
        byte = np.where(mant > 0.5, ex, ex - 1) + 127
    byte = np.clip(np.where(amax > 0, byte, 1), 1, 254)
    scaled = (w * np.exp2(127.0 - byte)[:, None, :]).reshape(k, n).astype(np.float32)
    by_word = np.ascontiguousarray(scaled.reshape(k // 512, 128, 4, n).transpose(0, 1, 3, 2))
    if fmt == "e4m3":
        words = by_word.astype(ml_dtypes.float8_e4m3fn).view(np.uint8)
    else:
        c = by_word.astype(ml_dtypes.float4_e2m1fn).view(np.uint8) & 0xF
        words = c[..., 0::2] | (c[..., 1::2] << 4)
    return np.ascontiguousarray(words), np.ascontiguousarray(byte.astype(np.uint8).reshape(k // 512, 16, n))


def unpack_weight(words, scales, fmt):
    g, p, n, _ = words.shape
    if fmt == "e4m3":
        vals = np.ascontiguousarray(words).view(ml_dtypes.float8_e4m3fn).astype(np.float64)
    else:
        nib = np.empty((g, p, n, 4), np.uint8)
        nib[..., 0::2] = words & 0xF
        nib[..., 1::2] = words >> 4
        vals = E2M1[nib]
    vals = vals * np.repeat(np.exp2(scales.astype(np.float64) - 127.0), 8, axis=1)[..., None]
    return vals.transpose(0, 1, 3, 2).reshape(g * 512, n)
def pack4(w):
    words, scales = pack_weight(w, "e2m1")
    return words.reshape(words.shape[0], 128, -1), scales


def unpack4(words, scales):
    return unpack_weight(words.reshape(words.shape[0], 128, -1, 2), scales, "e2m1")


R, L, C = 512, 1536, 2048

FAR_WEIGHT = 0.7
COUPLING = 0.2


def setup_inputs():
    s, u, t = mx_kscale(L), mx_kscale(C), mx_kscale(L)
    phi = np.random.standard_normal((R, L)) * s
    remote = np.random.standard_normal((R, C)) * u
    near = np.random.standard_normal((L, L)) / np.sqrt(L) / s[:, None] * t
    far = FAR_WEIGHT * np.random.standard_normal((C, L)) / np.sqrt(C) / u[:, None] * t
    lam = COUPLING * (1 + 0.1 * np.random.standard_normal(L)) / (s * s * s) * t
    acc = np.random.standard_normal((L, L)) / np.sqrt(L) / t[:, None]
    mom = np.random.standard_normal((R, L))
    far_words, far_scales = pack4(far)
    acc_words, acc_scales = pack4(acc)
    return {"phi": bf(phi), "remote": bf(remote), "near": bf(near),
            "far_words": far_words, "far_scales": far_scales, "lam": bf(lam),
            "acc_words": acc_words, "acc_scales": acc_scales, "mom": bf(mom)}


def reference(phi, remote, near, far_words, far_scales, lam, acc_words, acc_scales, mom):
    phi = f64(phi)
    linear = ((mxq(phi, 1, "e4m3") @ mxq(f64(near), 0, "e4m3"))
              + (mxq(f64(remote), 1, "e4m3") @ unpack4(far_words, far_scales)))
    force = linear - f64(lam) * (phi * phi * phi)
    return f64(mom) + (mxq(force, 1, "e4m3") @ unpack4(acc_words, acc_scales))

@@ -1,0 +1,490 @@
+from contextlib import ExitStack
+
+import concourse.mybir as mybir
+from concourse.masks import make_identity
+
+R, L, C = 512, 1536, 2048
+FLOPS = 2 * R * L * (L + C + L)
+
+F32 = mybir.dt.float32
+BF16 = mybir.dt.bfloat16
+U32 = mybir.dt.uint32
+I32 = mybir.dt.int32
+U8 = mybir.dt.uint8
+FP8X4 = mybir.dt.float8_e4m3fn_x4
+FP4X4 = mybir.dt.float4_e2m1fn_x4
+ALU = mybir.AluOpType
+ACT = mybir.ActivationFunctionType
+
+P = 128
+KP = 512
+NT = 512
+RT = R // P
+GL = L // KP
+GC = C // KP
+NC = L // NT
+WEAVE_V = (192, 192, 192)
+
+
+def tile_nonlocal_phi_four_kick_s3_kernel(
+    tc, phi, remote, near, far_words, far_scales, lam, acc_words, acc_scales, mom, out
+):
+    nc = tc.nc
+    with ExitStack() as ctx:
+        keep = ctx.enter_context(tc.tile_pool(name="keep", bufs=1))
+        stage = ctx.enter_context(tc.tile_pool(name="stage", bufs=3))
+        psum = ctx.enter_context(tc.psum_pool(name="psum", bufs=1))
+        ctx.enter_context(tc.manual_schedule())
+
+        t = {}
+
+        def bank(k, name):
+            return psum.tile([P, NT], F32, name=name, tag="bank%d" % k)
+
+        def load_lam():
+            t["lam_col"] = keep.tile([P, 6], F32, name="lam_col")
+            with nc.allow_non_contiguous_dma(reason="lam as one word a partition"):
+                nc.sync.dma_start(out=t["lam_col"][:], in_=lam.bitcast(F32).rearrange("(m p) -> p m", p=P))
+
+        def load_phi(i):
+            t["phi", i] = keep.tile([P, L], BF16, name="phi%d" % i)
+            nc.sync.dma_start(out=t["phi", i][:], in_=phi[i * P:(i + 1) * P, :])
+
+        def load_remote(i):
+            t["rem", i] = keep.tile([P, C], BF16, name="rem%d" % i, tag="rows%d" % i)
+            nc.sync.dma_start(out=t["rem", i][:], in_=remote[i * P:(i + 1) * P, :])
+
+        def load_mom(i):
+            t["mom", i] = keep.tile([P, L], BF16, name="mom%d" % i, tag="rows%d" % i)
+            nc.sync.dma_start(out=t["mom", i][:], in_=mom[i * P:(i + 1) * P, :])
+
+        def load_near(g, c0, c1):
+            raw = keep.tile([P, 4, (c1 - c0) * NT], BF16, name="near_raw%d_%d" % (g, c0))
+            rows = near[g * KP:(g + 1) * KP, c0 * NT:c1 * NT]
+            nc.sync.dma_start(out=raw[:], in_=rows.rearrange("(p j) n -> p j n", j=4))
+            for c in range(c0, c1):
+                t["near_raw", g, c] = raw[:, :, (c - c0) * NT:(c - c0 + 1) * NT]
+
+        def load_far(c0, c1):
+            w = keep.tile([P, GC, (c1 - c0) * 2 * NT], U8, name="far%d" % c0, align_bytes=64)
+            src = far_words.rearrange("g p b -> p g b")[:, :, c0 * 2 * NT:c1 * 2 * NT]
+            nc.sync.dma_start(out=w[:].bitcast(I32), in_=src.bitcast(I32))
+            for c in range(c0, c1):
+                t["far", c] = w[:, :, (c - c0) * 2 * NT:(c - c0 + 1) * 2 * NT]
+
+        def load_acc():
+            t["acc"] = keep.tile([P, GL, 2 * L], U8, name="acc", align_bytes=64)
+            nc.sync.dma_start(out=t["acc"][:].bitcast(I32), in_=acc_words.rearrange("g p b -> p g b").bitcast(I32))
+
+        def clear_plane(key, groups, width, eng):
+            t[key] = keep.tile([P, groups, width], U8, name=key, align_bytes=64)
+            eng.memset(t[key][:].bitcast(I32), 0)
+
+        def load_plane(key, scales, c0, c1):
+            for q in range(4):
+                nc.sync.dma_start(
+                    out=t[key][32 * q:32 * q + 4, :, :].bitcast(I32),
+                    in_=scales[:, 4 * q:4 * q + 4, c0 * NT:c1 * NT].rearrange("g r n -> r g n").bitcast(I32),
+                )
+
+        def spread_lam(k0, k1):
+            t["lam"] = keep.tile([P, NC, 2, P], F32, name="lam_rows")
+            for k, ms in ((k0, range(0, 4)), (k1, range(4, 6))):
+                b = bank(k, "lam_ps%d" % k)
+                for m in ms:
+                    j = m - ms.start
+                    nc.tensor.transpose(b[:, j * P:(j + 1) * P], t["lam_col"][:, m:m + 1].to_broadcast([P, P]), t["ident"][:])
+                n = len(ms) // 2
+                nc.scalar.copy(
+                    out=t["lam"][:, ms.start // 2:ms.start // 2 + n, :, :],
+                    in_=b[:, 0:n * 2 * P].rearrange("q (c p u) -> q c u p", u=2, p=P),
+                )
+
+        def turn(key, items, k, evac):
+            b = bank(k, "tr_%s" % key)
+            for j, (name, words) in enumerate(items):
+                for u in range(2):
+                    nc.tensor.transpose(b[:, (2 * j + u) * P:(2 * j + u + 1) * P], words[:, u, :], t["ident"][:])
+            t["turned", key] = (b, [name for name, words in items])
+
+        def gather(key):
+            b, names = t["turned", key]
+            n = len(names)
+            grouped = stage.tile([P, 2 * KP], BF16, name="grp_%s" % key, tag="grouped", bufs=4, align_bytes=64)
+            dst = grouped[:, 0:n * KP].bitcast(F32).rearrange("p (j r u) -> p j r u", j=n, u=2)
+            src = b[:, 0:n * 2 * P].rearrange("p (j u r) -> p j r u", j=n, u=2)
+            nc.scalar.copy(out=dst, in_=src)
+            t["grouped", key] = (grouped, names)
+
+        def quant_turned(key):
+            grouped, names = t["grouped", key]
+            n = len(names)
+            codes = keep.tile([P, n * P], U32, name="codes_%s" % key, align_bytes=64)
+            plane = keep.tile([P, n * P], U8, name="plane_%s" % key, align_bytes=64)
+            nc.vector.quantize_mx(out=codes[:].bitcast(FP8X4), scales=plane[:], in_=grouped[:, 0:n * KP])
+            for j, name in enumerate(names):
+                t[name] = (codes[:, j * P:(j + 1) * P], plane[:, j * P:(j + 1) * P])
+
+        def row_words(src, i, g):
+            words = t[src, i][:].bitcast(F32)[:, g * 2 * P:(g + 1) * 2 * P]
+            return (("q" + src, i, g), words.rearrange("r (p u) -> r u p", u=2))
+
+        def turn_phi(b, k, evac="S"):
+            turn("phi%d" % b, [row_words("phi", n // GL, n % GL) for n in (2 * b, 2 * b + 1)], k, evac)
+
+        def turn_rem(i, h, k, evac="S"):
+            turn("rem%d_%d" % (i, h), [row_words("rem", i, g) for g in (2 * h, 2 * h + 1)], k, evac)
+
+        def turn_force(c, rows, k, evac="S"):
+            items = []
+            for i in rows:
+                words = t["force", i, c][:].bitcast(F32).rearrange("r (u p) -> r u p", u=2)
+                items.append((("qforce", i, c), words))
+            turn("force%d_%d" % (c, rows[0]), items, k, evac)
+
+        def weave(g, c, eng):
+            if ("woven", g, c) not in t:
+                t["woven", g, c] = stage.tile([P, NT, 4], BF16, name="woven%d_%d" % (g, c), tag="woven", bufs=3, align_bytes=64)
+            cut = WEAVE_V[c]
+            cols = slice(cut, NT) if eng == "S" else slice(0, cut)
+            dst = t["woven", g, c][:, cols, :].rearrange("p (a i) j -> p a j i", i=4)
+            src = t["near_raw", g, c][:, :, cols].rearrange("p j (a i) -> p a j i", i=4)
+            if eng == "S":
+                nc.scalar.copy(out=dst, in_=src)
+            else:
+                nc.vector.tensor_copy(out=dst, in_=src)
+
+        def quant_near(g, c):
+            codes = keep.tile([P, NT], U32, name="near_codes%d_%d" % (g, c), align_bytes=64)
+            plane = keep.tile([P, NT], U8, name="near_plane%d_%d" % (g, c), align_bytes=64)
+            nc.vector.quantize_mx(
+                out=codes[:].bitcast(FP8X4), scales=plane[:], in_=t["woven", g, c][:].rearrange("p n j -> p (n j)")
+            )
+            t["qnear", g, c] = (codes, plane)
+
+        def sorted_phi(i, c):
+            return t["phi", i][:, c * NT:(c + 1) * NT].rearrange("r (p u e) -> r u p e", u=2, e=2)
+
+        def square(i, c):
+            sq = stage.tile([P, 2, P, 2], F32, name="sq%d_%d" % (i, c), tag="sq", bufs=4)
+            nc.scalar.activation(out=sq[:], in_=sorted_phi(i, c), func=ACT.Square)
+            t["sq", i, c] = sq
+
+        def couple(i, c):
+            cub = keep.tile([P, 2, P, 2], F32, name="cubic%d_%d" % (i, c))
+            lam_c = t["lam"][:, c, :, :].rearrange("q u p -> q (u p)").bitcast(BF16).rearrange("q (u p e) -> q u p e", u=2, e=2)
+            nc.vector.tensor_tensor(out=cub[:], in0=sorted_phi(i, c), in1=lam_c, op=ALU.mult)
+            t["cubic", i, c] = cub
+
+        def cube(i, c):
+            cub = t["cubic", i, c]
+            nc.vector.tensor_tensor(out=cub[:], in0=cub[:], in1=t["sq", i, c][:], op=ALU.mult)
+
+        def open_group(i, c, k):
+            t["lin", i, c] = bank(k, "lin%d_%d" % (i, c))
+            t["passes", i, c] = 0
+
+        def stage1_pass(i, c, lhs, rhs, rhs_scale):
+            n = t["passes", i, c]
+            nc.tensor.matmul_mx(
+                out=t["lin", i, c][:], lhsT=lhs[0].bitcast(FP8X4), lhsT_scale=lhs[1], rhs=rhs, rhs_scale=rhs_scale,
+                start=(n == 0), stop=(n == GL + GC - 1),
+            )
+            t["passes", i, c] = n + 1
+
+        def near_pass(i, c, g):
+            codes, plane = t["qnear", g, c]
+            stage1_pass(i, c, t["qphi", i, g], codes[:].bitcast(FP8X4), plane[:])
+
+        def far_pass(i, c, g):
+            stage1_pass(i, c, t["qrem", i, g], t["far", c][:, g, :].bitcast(FP4X4), t["far_plane0"][:, g, :] if c == 0 else t["far_plane1"][:, g, (c - 1) * NT:c * NT])
+
+        def far_passes(i, c):
+            for g in range(GC):
+                far_pass(i, c, g)
+
+        def near_passes(i, c):
+            for g in range(GL):
+                near_pass(i, c, g)
+
+        def force(i, c):
+            f = stage.tile([P, NT], BF16, name="force%d_%d" % (i, c), tag="force", bufs=4)
+            nc.vector.tensor_tensor(
+                out=f[:].rearrange("r (u p e) -> r u p e", u=2, e=2),
+                in0=t["lin", i, c][:].rearrange("r (p u e) -> r u p e", u=2, e=2),
+                in1=t["cubic", i, c][:], op=ALU.subtract,
+            )
+            t["force", i, c] = f
+
+        def kick_pass(i, m, g, k):
+            if g == 0:
+                t["kick", i, m] = bank(k, "kick%d_%d" % (i, m))
+            codes, plane = t["qforce", i, g]
+            nc.tensor.matmul_mx(
+                out=t["kick", i, m][:], lhsT=codes.bitcast(FP8X4), lhsT_scale=plane,
+                rhs=t["acc"][:, g, m * 2 * NT:(m + 1) * 2 * NT].bitcast(FP4X4),
+                rhs_scale=t["acc_plane"][:, g, m * NT:(m + 1) * NT],
+                start=(g == 0), stop=(g == GL - 1),
+            )
+
+        def kick(i, m, k):
+            for g in range(GL):
+                kick_pass(i, m, g, k)
+
+        def kick_by_pass(i, ks, gs):
+            for g in gs:
+                for m in range(NC):
+                    kick_pass(i, m, g, ks[m])
+
+        def turn_phi_row(i, k0, k1):
+            turn("phi%d_0" % i, [row_words("phi", i, 0), row_words("phi", i, 1)], k0, "S")
+            turn("phi%d_1" % i, [row_words("phi", i, 2)], k1, "S")
+
+        def finish(i, m):
+            res = stage.tile([P, NT], F32, name="res%d_%d" % (i, m), tag="res", bufs=5)
+            nc.vector.tensor_tensor(out=res[:], in0=t["kick", i, m][:], in1=t["mom", i][:, m * NT:(m + 1) * NT], op=ALU.add)
+            nc.sync.dma_start(out=out[i * P:(i + 1) * P, m * NT:(m + 1) * NT], in_=res[:])
+
+        load_lam()
+        load_phi(0)
+        load_near(0,0,1)
+        load_phi(1)
+
+        clear_plane("far_plane0", GC, NT, nc.vector)
+        clear_plane("far_plane1", GC, 2 * NT, nc.vector)
+        t["ident"] = keep.tile([P, P], F32, name="ident")
+        make_identity(nc, t["ident"][:])
+        clear_plane("acc_plane", GL, L, nc.gpsimd)
+        load_remote(0)
+        load_plane("far_plane0", far_scales, 0, 1)
+        load_far(0, 1)
+        load_phi(2)
+        load_phi(3)
+        load_near(1,0,1)
+        load_remote(1)
+        load_remote(2)
+        load_near(2,0,1)
+        load_remote(3)
+        load_near(0, 1, 3)
+        load_plane("far_plane1", far_scales, 1, 3)
+        load_far(1, 3)
+        load_near(1, 1, 3)
+        load_near(2, 1, 3)
+        load_plane("acc_plane", acc_scales, 0, 3)
+        load_acc()
+        spread_lam(0,1)
+        turn_phi(0,4)
+        turn_phi(1,5)
+        turn_phi(2,6)
+        turn_rem(0,0,7)
+        gather("phi0")
+        weave(0,0,"S")
+        gather("phi1")
+        gather("phi2")
+        gather("rem0_0")
+        couple(0,0)
+        weave(0,0,"V")
+        quant_turned("phi0")
+        couple(0,1)
+        couple(1,0)
+        quant_near(0,0)
+        quant_turned("phi1")
+        quant_turned("phi2")
+        couple(1,1)
+        quant_turned("rem0_0")
+        turn_rem(0,1,4)
+        open_group(0,0,0)
+        open_group(1,0,1)
+        near_pass(0,0,0)
+        near_pass(1,0,0)
+        turn_phi(3,5)
+        turn_phi(4,6)
+        turn_phi(5,7)
+        gather("rem0_1")
+        square(0,0)
+        square(1,0)
+        gather("phi3")
+        gather("phi4")
+        gather("phi5")
+        weave(1,0,"S")
+        square(2,0)
+        quant_turned("rem0_1")
+        couple(0,2)
+        cube(0,0)
+        couple(2,0)
+        quant_turned("phi3")
+        cube(1,0)
+        quant_turned("phi4")
+        weave(1,0,"V")
+        quant_turned("phi5")
+        couple(3,0)
+        couple(2,1)
+        quant_near(1,0)
+        cube(2,0)
+        load_mom(0)
+        far_passes(0,0)
+        turn_rem(1,0,4)
+        turn_rem(1,1,5)
+        open_group(2,0,2)
+        open_group(3,0,3)
+        near_pass(2,0,0)
+        near_pass(3,0,0)
+        turn_rem(2,0,6)
+        turn_rem(2,1,7)
+        near_pass(0,0,1)
+        near_pass(1,0,1)
+        near_pass(2,0,1)
+        near_pass(3,0,1)
+        gather("rem1_0")
+        gather("rem1_1")
+        weave(2,0,"S")
+        gather("rem2_0")
+        gather("rem2_1")
+        square(3,0)
+        weave(0,1,"S")
+        quant_turned("rem1_0")
+        quant_turned("rem1_1")
+        weave(2,0,"V")
+        couple(3,1)
+        couple(1,2)
+        quant_near(2,0)
+        quant_turned("rem2_0")
+        quant_turned("rem2_1")
+        weave(0,1,"V")
+        cube(3,0)
+        couple(2,2)
+        quant_near(0,1)
+        load_mom(1)
+        load_mom(2)
+        far_passes(1,0)
+        turn_rem(3,0,4)
+        turn_rem(3,1,5)
+        near_pass(0,0,2)
+        near_pass(1,0,2)
+        far_passes(2,0)
+        near_pass(2,0,2)
+        near_pass(3,0,2)
+        gather("rem3_0")
+        gather("rem3_1")
+        weave(0,2,"S")
+        square(0,1)
+        square(1,1)
+        weave(1,1,"S")
+        square(2,1)
+        square(3,1)
+        weave(2,1,"S")
+        quant_turned("rem3_0")
+        quant_turned("rem3_1")
+        weave(0,2,"V")
+        force(0,0)
+        force(1,0)
+        force(2,0)
+        quant_near(0,2)
+        load_mom(3)
+        far_passes(3,0)
+        open_group(0,1,6)
+        far_passes(0,1)
+        open_group(1,1,7)
+        far_passes(1,1)
+        open_group(2,1,4)
+        far_passes(2,1)
+        open_group(3,1,5)
+        far_passes(3,1)
+        turn_force(0,(0,1),0)
+        weave(1,2,"S")
+        force(3,0)
+        weave(1,1,"V")
+        cube(0,1)
+        cube(1,1)
+        quant_near(1,1)
+        weave(2,1,"V")
+        weave(1,2,"V")
+        cube(2,1)
+        cube(3,1)
+        quant_near(2,1)
+        couple(3,2)
+        weave(2,2,"V")
+        quant_near(1,2)
+        turn_force(0,(2,3),1)
+        near_pass(0,1,0)
+        near_pass(1,1,0)
+        near_pass(2,1,0)
+        near_pass(3,1,0)
+        near_pass(0,1,1)
+        near_pass(1,1,1)
+        near_pass(2,1,1)
+        near_pass(3,1,1)
+        near_pass(0,1,2)
+        near_pass(1,1,2)
+        near_pass(2,1,2)
+        near_pass(3,1,2)
+        open_group(0,2,2)
+        far_passes(0,2)
+        open_group(1,2,3)
+        far_passes(1,2)
+        weave(2,2,"S")
+        gather("force0_0")
+        gather("force0_2")
+        square(0,2)
+        square(1,2)
+        square(2,2)
+        square(3,2)
+        force(0,1)
+        force(1,1)
+        quant_near(2,2)
+        force(2,1)
+        force(3,1)
+        quant_turned("force0_0")
+        cube(0,2)
+        cube(1,2)
+        near_passes(0,2)
+        near_passes(1,2)
+        turn_force(1,(0,1),6)
+        turn_force(1,(2,3),7)
+        open_group(2,2,0)
+        far_passes(2,2)
+        near_passes(2,2)
+        gather("force1_0")
+        gather("force1_2")
+        force(0,2)
+        force(1,2)
+        cube(2,2)
+        quant_turned("force1_0")
+        cube(3,2)
+        quant_turned("force0_2")
+        force(2,2)
+        quant_turned("force1_2")
+        turn_force(2,(0,1),4)
+        open_group(3,2,1)
+        far_passes(3,2)
+        near_passes(3,2)
+        gather("force2_0")
+        quant_turned("force2_0")
+        force(3,2)
+        kick(0,0,5)
+        kick(0,1,2)
+        kick(0,2,3)
+        turn_force(2,(2,3),4)
+        kick(1,0,6)
+        kick(1,1,7)
+        gather("force2_2")
+        finish(0,0)
+        finish(0,1)
+        finish(0,2)
+        quant_turned("force2_2")
+        finish(1,0)
+        finish(1,1)
+        kick(1,2,5)
+        kick(2,0,2)
+        kick(2,1,3)
+        kick(2,2,6)
+        kick(3,0,7)
+        finish(1,2)
+        finish(2,0)
+        finish(2,1)
+        finish(2,2)
+        finish(3,0)
+        kick(3,1,5)
+        kick(3,2,2)
+        finish(3,1)
+        finish(3,2)

@@ -23,7 +23,7 @@ RT = R // P
 GL = L // KP
 GC = C // KP
 NC = L // NT
-WEAVE_V = (192, 192, 192)
+WEAVE_V = (256, 160, 160)
 
 
 def tile_nonlocal_phi_four_kick_s3_kernel(
@@ -42,9 +42,9 @@ def tile_nonlocal_phi_four_kick_s3_kernel(
             return psum.tile([P, NT], F32, name=name, tag="bank%d" % k)
 
         def load_lam():
-            t["lam_col"] = keep.tile([P, 6], F32, name="lam_col")
+            t["lam_col"] = keep.tile([P, NC, 2], F32, name="lam_col")
             with nc.allow_non_contiguous_dma(reason="lam as one word a partition"):
-                nc.sync.dma_start(out=t["lam_col"][:], in_=lam.bitcast(F32).rearrange("(m p) -> p m", p=P))
+                nc.scalar.dma_start(out=t["lam_col"][:], in_=lam.bitcast(F32).rearrange("(c p u) -> p c u", p=P, u=2))
 
         def load_phi(i):
             t["phi", i] = keep.tile([P, L], BF16, name="phi%d" % i)
@@ -65,12 +65,12 @@ def tile_nonlocal_phi_four_kick_s3_kernel(
             for c in range(c0, c1):
                 t["near_raw", g, c] = raw[:, :, (c - c0) * NT:(c - c0 + 1) * NT]
 
-        def load_far(c0, c1):
-            w = keep.tile([P, GC, (c1 - c0) * 2 * NT], U8, name="far%d" % c0, align_bytes=64)
-            src = far_words.rearrange("g p b -> p g b")[:, :, c0 * 2 * NT:c1 * 2 * NT]
+        def load_far(c, g0, g1):
+            w = keep.tile([P, g1 - g0, 2 * NT], U8, name="far%d_%d" % (c, g0), align_bytes=64)
+            src = far_words.rearrange("g p b -> p g b")[:, g0:g1, c * 2 * NT:(c + 1) * 2 * NT]
             nc.sync.dma_start(out=w[:].bitcast(I32), in_=src.bitcast(I32))
-            for c in range(c0, c1):
-                t["far", c] = w[:, :, (c - c0) * 2 * NT:(c - c0 + 1) * 2 * NT]
+            for g in range(g0, g1):
+                t["far", c, g] = w[:, g - g0, :]
 
         def load_acc():
             t["acc"] = keep.tile([P, GL, 2 * L], U8, name="acc", align_bytes=64)
@@ -87,18 +87,19 @@ def tile_nonlocal_phi_four_kick_s3_kernel(
                     in_=scales[:, 4 * q:4 * q + 4, c0 * NT:c1 * NT].rearrange("g r n -> r g n").bitcast(I32),
                 )
 
-        def spread_lam(k0, k1):
-            t["lam"] = keep.tile([P, NC, 2, P], F32, name="lam_rows")
-            for k, ms in ((k0, range(0, 4)), (k1, range(4, 6))):
-                b = bank(k, "lam_ps%d" % k)
-                for m in ms:
-                    j = m - ms.start
-                    nc.tensor.transpose(b[:, j * P:(j + 1) * P], t["lam_col"][:, m:m + 1].to_broadcast([P, P]), t["ident"][:])
-                n = len(ms) // 2
-                nc.scalar.copy(
-                    out=t["lam"][:, ms.start // 2:ms.start // 2 + n, :, :],
-                    in_=b[:, 0:n * 2 * P].rearrange("q (c p u) -> q c u p", u=2, p=P),
-                )
+        def spread_lam(c0, c1, k):
+            b = bank(k, "lam_ps%d" % c0)
+            for m in range(2 * c0, 2 * c1):
+                j = m - 2 * c0
+                nc.tensor.transpose(b[:, j * P:(j + 1) * P], t["lam_col"][:, m // 2, m % 2:m % 2 + 1].to_broadcast([P, P]), t["ident"][:])
+            t["lam_ps", c0] = (b, c1)
+
+        def gather_lam(c0):
+            b, c1 = t["lam_ps", c0]
+            rows = keep.tile([P, c1 - c0, 2, P], F32, name="lam_rows%d" % c0)
+            nc.scalar.copy(out=rows[:], in_=b[:, 0:(c1 - c0) * 2 * P].rearrange("q (c u p) -> q c u p", u=2, p=P))
+            for c in range(c0, c1):
+                t["lam", c] = rows[:, c - c0, :, :]
 
         def turn(key, items, k, evac):
             b = bank(k, "tr_%s" % key)
@@ -172,7 +173,7 @@ def tile_nonlocal_phi_four_kick_s3_kernel(
 
         def couple(i, c):
             cub = keep.tile([P, 2, P, 2], F32, name="cubic%d_%d" % (i, c))
-            lam_c = t["lam"][:, c, :, :].rearrange("q u p -> q (u p)").bitcast(BF16).rearrange("q (u p e) -> q u p e", u=2, e=2)
+            lam_c = t["lam", c].rearrange("q u p -> q (u p)").bitcast(BF16).rearrange("q (u p e) -> q u p e", u=2, e=2)
             nc.vector.tensor_tensor(out=cub[:], in0=sorted_phi(i, c), in1=lam_c, op=ALU.mult)
             t["cubic", i, c] = cub
 
@@ -197,7 +198,7 @@ def tile_nonlocal_phi_four_kick_s3_kernel(
             stage1_pass(i, c, t["qphi", i, g], codes[:].bitcast(FP8X4), plane[:])
 
         def far_pass(i, c, g):
-            stage1_pass(i, c, t["qrem", i, g], t["far", c][:, g, :].bitcast(FP4X4), t["far_plane0"][:, g, :] if c == 0 else t["far_plane1"][:, g, (c - 1) * NT:c * NT])
+            stage1_pass(i, c, t["qrem", i, g], t["far", c, g].bitcast(FP4X4), t["far_plane%d" % c][:, g, :])
 
         def far_passes(i, c):
             for g in range(GC):
@@ -208,7 +209,7 @@ def tile_nonlocal_phi_four_kick_s3_kernel(
                 near_pass(i, c, g)
 
         def force(i, c):
-            f = stage.tile([P, NT], BF16, name="force%d_%d" % (i, c), tag="force", bufs=4)
+            f = stage.tile([P, NT], BF16, name="force%d_%d" % (i, c), tag="force", bufs=8)
             nc.vector.tensor_tensor(
                 out=f[:].rearrange("r (u p e) -> r u p e", u=2, e=2),
                 in0=t["lin", i, c][:].rearrange("r (p u e) -> r u p e", u=2, e=2),
@@ -240,251 +241,189 @@ def tile_nonlocal_phi_four_kick_s3_kernel(
             turn("phi%d_0" % i, [row_words("phi", i, 0), row_words("phi", i, 1)], k0, "S")
             turn("phi%d_1" % i, [row_words("phi", i, 2)], k1, "S")
 
-        def finish(i, m):
-            res = stage.tile([P, NT], F32, name="res%d_%d" % (i, m), tag="res", bufs=5)
-            nc.vector.tensor_tensor(out=res[:], in0=t["kick", i, m][:], in1=t["mom", i][:, m * NT:(m + 1) * NT], op=ALU.add)
-            nc.sync.dma_start(out=out[i * P:(i + 1) * P, m * NT:(m + 1) * NT], in_=res[:])
+        def finish(i, m, parts=1):
+            width = NT // parts
+            for j in range(parts):
+                res = stage.tile([P, width], F32, name="res%d_%d_%d" % (i, m, j), tag="res", bufs=5)
+                cols = slice(m * NT + j * width, m * NT + (j + 1) * width)
+                nc.vector.tensor_tensor(out=res[:], in0=t["kick", i, m][:, j * width:(j + 1) * width], in1=t["mom", i][:, cols], op=ALU.add)
+                nc.sync.dma_start(out=out[i * P:(i + 1) * P, cols], in_=res[:])
+
+        def gather2(key):
+            gather(key + "_0")
+            gather(key + "_1")
+
+        def quant2(key):
+            quant_turned(key + "_0")
+            quant_turned(key + "_1")
+
+        def load_far_chunk(c):
+            load_plane("far_plane%d" % c, far_scales, c, c + 1)
+            load_far(c, 0, GC)
+
 
         load_lam()
         load_phi(0)
-        load_near(0,0,1)
-        load_phi(1)
-
-        clear_plane("far_plane0", GC, NT, nc.vector)
-        clear_plane("far_plane1", GC, 2 * NT, nc.vector)
+        load_remote(0)
+        load_remote(1)
         t["ident"] = keep.tile([P, P], F32, name="ident")
         make_identity(nc, t["ident"][:])
-        clear_plane("acc_plane", GL, L, nc.gpsimd)
-        load_remote(0)
+        for c in range(NC):
+            clear_plane("far_plane%d" % c, GC, NT, nc.vector)
+        clear_plane("acc_plane", GL, L, nc.vector)
         load_plane("far_plane0", far_scales, 0, 1)
-        load_far(0, 1)
-        load_phi(2)
-        load_phi(3)
-        load_near(1,0,1)
-        load_remote(1)
-        load_remote(2)
-        load_near(2,0,1)
-        load_remote(3)
-        load_near(0, 1, 3)
-        load_plane("far_plane1", far_scales, 1, 3)
-        load_far(1, 3)
-        load_near(1, 1, 3)
-        load_near(2, 1, 3)
+        load_far(0, 0, 2)
+        load_far(0, 2, GC)
+        for i in range(1, RT):
+            load_near(i - 1, 0, 1)
+            load_phi(i)
+            if i + 1 < RT:
+                load_remote(i + 1)
+        for c in range(1, NC):
+            load_near(0, c, c + 1)
+            load_far_chunk(c)
+            load_near(1, c, c + 1)
+            load_near(2, c, c + 1)
         load_plane("acc_plane", acc_scales, 0, 3)
         load_acc()
-        spread_lam(0,1)
-        turn_phi(0,4)
-        turn_phi(1,5)
-        turn_phi(2,6)
-        turn_rem(0,0,7)
-        gather("phi0")
-        weave(0,0,"S")
-        gather("phi1")
-        gather("phi2")
-        gather("rem0_0")
-        couple(0,0)
-        weave(0,0,"V")
-        quant_turned("phi0")
-        couple(0,1)
-        couple(1,0)
-        quant_near(0,0)
-        quant_turned("phi1")
-        quant_turned("phi2")
-        couple(1,1)
-        quant_turned("rem0_0")
-        turn_rem(0,1,4)
-        open_group(0,0,0)
-        open_group(1,0,1)
-        near_pass(0,0,0)
-        near_pass(1,0,0)
-        turn_phi(3,5)
-        turn_phi(4,6)
-        turn_phi(5,7)
-        gather("rem0_1")
-        square(0,0)
-        square(1,0)
-        gather("phi3")
-        gather("phi4")
-        gather("phi5")
-        weave(1,0,"S")
-        square(2,0)
-        quant_turned("rem0_1")
-        couple(0,2)
-        cube(0,0)
-        couple(2,0)
-        quant_turned("phi3")
-        cube(1,0)
-        quant_turned("phi4")
-        weave(1,0,"V")
-        quant_turned("phi5")
-        couple(3,0)
-        couple(2,1)
-        quant_near(1,0)
-        cube(2,0)
-        load_mom(0)
-        far_passes(0,0)
-        turn_rem(1,0,4)
-        turn_rem(1,1,5)
-        open_group(2,0,2)
-        open_group(3,0,3)
-        near_pass(2,0,0)
-        near_pass(3,0,0)
-        turn_rem(2,0,6)
-        turn_rem(2,1,7)
-        near_pass(0,0,1)
-        near_pass(1,0,1)
-        near_pass(2,0,1)
-        near_pass(3,0,1)
-        gather("rem1_0")
-        gather("rem1_1")
-        weave(2,0,"S")
-        gather("rem2_0")
-        gather("rem2_1")
-        square(3,0)
-        weave(0,1,"S")
-        quant_turned("rem1_0")
-        quant_turned("rem1_1")
-        weave(2,0,"V")
-        couple(3,1)
-        couple(1,2)
-        quant_near(2,0)
-        quant_turned("rem2_0")
-        quant_turned("rem2_1")
-        weave(0,1,"V")
-        cube(3,0)
-        couple(2,2)
-        quant_near(0,1)
-        load_mom(1)
-        load_mom(2)
-        far_passes(1,0)
-        turn_rem(3,0,4)
-        turn_rem(3,1,5)
-        near_pass(0,0,2)
-        near_pass(1,0,2)
-        far_passes(2,0)
-        near_pass(2,0,2)
-        near_pass(3,0,2)
-        gather("rem3_0")
-        gather("rem3_1")
-        weave(0,2,"S")
-        square(0,1)
-        square(1,1)
-        weave(1,1,"S")
-        square(2,1)
-        square(3,1)
-        weave(2,1,"S")
-        quant_turned("rem3_0")
-        quant_turned("rem3_1")
-        weave(0,2,"V")
-        force(0,0)
-        force(1,0)
-        force(2,0)
-        quant_near(0,2)
-        load_mom(3)
-        far_passes(3,0)
-        open_group(0,1,6)
-        far_passes(0,1)
-        open_group(1,1,7)
-        far_passes(1,1)
-        open_group(2,1,4)
-        far_passes(2,1)
-        open_group(3,1,5)
-        far_passes(3,1)
-        turn_force(0,(0,1),0)
-        weave(1,2,"S")
-        force(3,0)
-        weave(1,1,"V")
-        cube(0,1)
-        cube(1,1)
-        quant_near(1,1)
-        weave(2,1,"V")
-        weave(1,2,"V")
-        cube(2,1)
-        cube(3,1)
-        quant_near(2,1)
-        couple(3,2)
-        weave(2,2,"V")
-        quant_near(1,2)
-        turn_force(0,(2,3),1)
-        near_pass(0,1,0)
-        near_pass(1,1,0)
-        near_pass(2,1,0)
-        near_pass(3,1,0)
-        near_pass(0,1,1)
-        near_pass(1,1,1)
-        near_pass(2,1,1)
-        near_pass(3,1,1)
-        near_pass(0,1,2)
-        near_pass(1,1,2)
-        near_pass(2,1,2)
-        near_pass(3,1,2)
-        open_group(0,2,2)
-        far_passes(0,2)
-        open_group(1,2,3)
-        far_passes(1,2)
-        weave(2,2,"S")
+
+        spread_lam(0, 1, 3)
+        spread_lam(1, 3, 2)
+        gather_lam(0)
+        gather_lam(1)
+        for c in range(NC):
+            couple(0, c)
+        square(0, 0)
+        cube(0, 0)
+        turn_phi_row(0, 4, 5)
+        gather2("phi0")
+        quant2("phi0")
+        for i in range(2):
+            turn_rem(i, 0, 6 - 2 * i)
+            turn_rem(i, 1, 7 - 2 * i)
+            gather2("rem%d" % i)
+            quant2("rem%d" % i)
+        for c in range(1, NC):
+            square(0, c)
+        cube(0, 1)
+        for i in range(2):
+            open_group(i, 0, i)
+            far_pass(i, 0, 0)
+            far_pass(i, 0, 1)
+        far_pass(0, 0, 2)
+        far_pass(0, 0, 3)
+        done = []
+        for i in range(1, RT):
+            weave(i - 1, 0, "S")
+            weave(i - 1, 0, "V")
+            turn_phi_row(i, 6, 7)
+            gather2("phi%d" % i)
+            if i == 1:
+                cube(0, 2)
+            couple(i, 0)
+            quant_near(i - 1, 0)
+            quant2("phi%d" % i)
+            if i > 1:
+                open_group(i, 0, i)
+            for g in range(2 if i == 1 else 0, GC):
+                far_pass(i, 0, g)
+            square(i, 0)
+            if i + 1 < RT:
+                turn_rem(i + 1, 0, 4)
+                turn_rem(i + 1, 1, 5)
+                gather2("rem%d" % (i + 1))
+                if i == 1:
+                    couple(i, 1)
+                quant_turned("rem%d_0" % (i + 1))
+                cube(i, 0)
+                quant_turned("rem%d_1" % (i + 1))
+            for r in range(i + 1):
+                for g in range(i):
+                    if (r, g) not in done:
+                        near_pass(r, 0, g)
+                        done.append((r, g))
+        for i in range(RT):
+            load_mom(i)
+
+        for i in range(RT):
+            open_group(i, 1, 4 + i)
+            far_passes(i, 1)
+        for g in range(GL):
+            weave(g, 1, "S")
+            weave(g, 1, "V")
+            if g == 0:
+                cube(RT - 1, 0)
+            if g < 2:
+                force(2 * g, 0)
+                force(2 * g + 1, 0)
+            else:
+                couple(2, 1)
+                couple(3, 1)
+            quant_near(g, 1)
+            square(g + 1, 1)
+        turn_force(0, (0, 1), 0)
+        turn_force(0, (2, 3), 1)
+        for g in range(GL):
+            for i in range(RT):
+                near_pass(i, 1, g)
+        for g in range(GL):
+            weave(g, 2, "S")
+            weave(g, 2, "V")
+            cube(g + 1, 1)
+            quant_near(g, 2)
+        for i in range(2):
+            open_group(i, 2, 2 + i)
+            far_passes(i, 2)
+        for i in range(2):
+            near_passes(i, 2)
         gather("force0_0")
+        square(1, 2)
         gather("force0_2")
-        square(0,2)
-        square(1,2)
-        square(2,2)
-        square(3,2)
-        force(0,1)
-        force(1,1)
-        quant_near(2,2)
-        force(2,1)
-        force(3,1)
+        square(2, 2)
+        square(3, 2)
+        force(0, 1)
+        force(1, 1)
+        couple(1, 2)
+        force(2, 1)
+        force(3, 1)
+        cube(1, 2)
+        force(0, 2)
+        force(1, 2)
         quant_turned("force0_0")
-        cube(0,2)
-        cube(1,2)
-        near_passes(0,2)
-        near_passes(1,2)
-        turn_force(1,(0,1),6)
-        turn_force(1,(2,3),7)
-        open_group(2,2,0)
-        far_passes(2,2)
-        near_passes(2,2)
-        gather("force1_0")
-        gather("force1_2")
-        force(0,2)
-        force(1,2)
-        cube(2,2)
-        quant_turned("force1_0")
-        cube(3,2)
+        open_group(2, 2, 0)
+        far_passes(2, 2)
+        near_passes(2, 2)
+        open_group(3, 2, 1)
+        far_passes(3, 2)
+        turn_force(1, (0, 1), 4)
+        turn_force(2, (0, 1), 5)
+        turn_force(1, (2, 3), 6)
+        near_passes(3, 2)
+        couple(2, 2)
         quant_turned("force0_2")
-        force(2,2)
-        quant_turned("force1_2")
-        turn_force(2,(0,1),4)
-        open_group(3,2,1)
-        far_passes(3,2)
-        near_passes(3,2)
+        couple(3, 2)
+        gather("force1_0")
         gather("force2_0")
+        gather("force1_2")
+        quant_turned("force1_0")
+        cube(2, 2)
         quant_turned("force2_0")
-        force(3,2)
-        kick(0,0,5)
-        kick(0,1,2)
-        kick(0,2,3)
-        turn_force(2,(2,3),4)
-        kick(1,0,6)
-        kick(1,1,7)
+        cube(3, 2)
+        force(2, 2)
+        force(3, 2)
+        quant_turned("force1_2")
+        kick_by_pass(0, (7, 2, 3), (0, 1, 2))
+        for m in range(NC):
+            finish(0, m)
+        for m in range(2):
+            kick(1, m, 4 + m)
+            finish(1, m)
+        turn_force(2, (2, 3), 0)
         gather("force2_2")
-        finish(0,0)
-        finish(0,1)
-        finish(0,2)
         quant_turned("force2_2")
-        finish(1,0)
-        finish(1,1)
-        kick(1,2,5)
-        kick(2,0,2)
-        kick(2,1,3)
-        kick(2,2,6)
-        kick(3,0,7)
-        finish(1,2)
-        finish(2,0)
-        finish(2,1)
-        finish(2,2)
-        finish(3,0)
-        kick(3,1,5)
-        kick(3,2,2)
-        finish(3,1)
-        finish(3,2)
+        kick(1, 2, 6)
+        finish(1, 2)
+        for i in range(2, RT):
+            for m in range(NC):
+                kick(i, m, ((7, 2, 3), (1, 4, 5))[i - 2][m])
+                finish(i, m, 2 if (i, m) == (RT - 1, NC - 1) else 1)

from contextlib import ExitStack

import concourse.mybir as mybir
from concourse.masks import make_identity

R, L, C = 512, 1536, 2048
FLOPS = 2 * R * L * (L + C + L)

F32 = mybir.dt.float32
BF16 = mybir.dt.bfloat16
U32 = mybir.dt.uint32
I32 = mybir.dt.int32
U8 = mybir.dt.uint8
FP8X4 = mybir.dt.float8_e4m3fn_x4
FP4X4 = mybir.dt.float4_e2m1fn_x4
ALU = mybir.AluOpType
ACT = mybir.ActivationFunctionType

P = 128
KP = 512
NT = 512
RT = R // P
GL = L // KP
GC = C // KP
NC = L // NT
WEAVE_V = (256, 160, 160)


def tile_nonlocal_phi_four_kick_s3_kernel(
    tc, phi, remote, near, far_words, far_scales, lam, acc_words, acc_scales, mom, out
):
    nc = tc.nc
    with ExitStack() as ctx:
        keep = ctx.enter_context(tc.tile_pool(name="keep", bufs=1))
        stage = ctx.enter_context(tc.tile_pool(name="stage", bufs=3))
        psum = ctx.enter_context(tc.psum_pool(name="psum", bufs=1))
        ctx.enter_context(tc.manual_schedule())

        t = {}

        def bank(k, name):
            return psum.tile([P, NT], F32, name=name, tag="bank%d" % k)

        def load_lam():
            t["lam_col"] = keep.tile([P, NC, 2], F32, name="lam_col")
            with nc.allow_non_contiguous_dma(reason="lam as one word a partition"):
                nc.scalar.dma_start(out=t["lam_col"][:], in_=lam.bitcast(F32).rearrange("(c p u) -> p c u", p=P, u=2))

        def load_phi(i):
            t["phi", i] = keep.tile([P, L], BF16, name="phi%d" % i)
            nc.sync.dma_start(out=t["phi", i][:], in_=phi[i * P:(i + 1) * P, :])

        def load_remote(i):
            t["rem", i] = keep.tile([P, C], BF16, name="rem%d" % i, tag="rows%d" % i)
            nc.sync.dma_start(out=t["rem", i][:], in_=remote[i * P:(i + 1) * P, :])

        def load_mom(i):
            t["mom", i] = keep.tile([P, L], BF16, name="mom%d" % i, tag="rows%d" % i)
            nc.sync.dma_start(out=t["mom", i][:], in_=mom[i * P:(i + 1) * P, :])

        def load_near(g, c0, c1):
            raw = keep.tile([P, 4, (c1 - c0) * NT], BF16, name="near_raw%d_%d" % (g, c0))
            rows = near[g * KP:(g + 1) * KP, c0 * NT:c1 * NT]
            nc.sync.dma_start(out=raw[:], in_=rows.rearrange("(p j) n -> p j n", j=4))
            for c in range(c0, c1):
                t["near_raw", g, c] = raw[:, :, (c - c0) * NT:(c - c0 + 1) * NT]

        def load_far(c, g0, g1):
            w = keep.tile([P, g1 - g0, 2 * NT], U8, name="far%d_%d" % (c, g0), align_bytes=64)
            src = far_words.rearrange("g p b -> p g b")[:, g0:g1, c * 2 * NT:(c + 1) * 2 * NT]
            nc.sync.dma_start(out=w[:].bitcast(I32), in_=src.bitcast(I32))
            for g in range(g0, g1):
                t["far", c, g] = w[:, g - g0, :]

        def load_acc():
            t["acc"] = keep.tile([P, GL, 2 * L], U8, name="acc", align_bytes=64)
            nc.sync.dma_start(out=t["acc"][:].bitcast(I32), in_=acc_words.rearrange("g p b -> p g b").bitcast(I32))

        def clear_plane(key, groups, width, eng):
            t[key] = keep.tile([P, groups, width], U8, name=key, align_bytes=64)
            eng.memset(t[key][:].bitcast(I32), 0)

        def load_plane(key, scales, c0, c1):
            for q in range(4):
                nc.sync.dma_start(
                    out=t[key][32 * q:32 * q + 4, :, :].bitcast(I32),
                    in_=scales[:, 4 * q:4 * q + 4, c0 * NT:c1 * NT].rearrange("g r n -> r g n").bitcast(I32),
                )

        def spread_lam(c0, c1, k):
            b = bank(k, "lam_ps%d" % c0)
            for m in range(2 * c0, 2 * c1):
                j = m - 2 * c0
                nc.tensor.transpose(b[:, j * P:(j + 1) * P], t["lam_col"][:, m // 2, m % 2:m % 2 + 1].to_broadcast([P, P]), t["ident"][:])
            t["lam_ps", c0] = (b, c1)

        def gather_lam(c0):
            b, c1 = t["lam_ps", c0]
            rows = keep.tile([P, c1 - c0, 2, P], F32, name="lam_rows%d" % c0)
            nc.scalar.copy(out=rows[:], in_=b[:, 0:(c1 - c0) * 2 * P].rearrange("q (c u p) -> q c u p", u=2, p=P))
            for c in range(c0, c1):
                t["lam", c] = rows[:, c - c0, :, :]

        def turn(key, items, k, evac):
            b = bank(k, "tr_%s" % key)
            for j, (name, words) in enumerate(items):
                for u in range(2):
                    nc.tensor.transpose(b[:, (2 * j + u) * P:(2 * j + u + 1) * P], words[:, u, :], t["ident"][:])
            t["turned", key] = (b, [name for name, words in items])

        def gather(key):
            b, names = t["turned", key]
            n = len(names)
            grouped = stage.tile([P, 2 * KP], BF16, name="grp_%s" % key, tag="grouped", bufs=4, align_bytes=64)
            dst = grouped[:, 0:n * KP].bitcast(F32).rearrange("p (j r u) -> p j r u", j=n, u=2)
            src = b[:, 0:n * 2 * P].rearrange("p (j u r) -> p j r u", j=n, u=2)
            nc.scalar.copy(out=dst, in_=src)
            t["grouped", key] = (grouped, names)

        def quant_turned(key):
            grouped, names = t["grouped", key]
            n = len(names)
            codes = keep.tile([P, n * P], U32, name="codes_%s" % key, align_bytes=64)
            plane = keep.tile([P, n * P], U8, name="plane_%s" % key, align_bytes=64)
            nc.vector.quantize_mx(out=codes[:].bitcast(FP8X4), scales=plane[:], in_=grouped[:, 0:n * KP])
            for j, name in enumerate(names):
                t[name] = (codes[:, j * P:(j + 1) * P], plane[:, j * P:(j + 1) * P])

        def row_words(src, i, g):
            words = t[src, i][:].bitcast(F32)[:, g * 2 * P:(g + 1) * 2 * P]
            return (("q" + src, i, g), words.rearrange("r (p u) -> r u p", u=2))

        def turn_phi(b, k, evac="S"):
            turn("phi%d" % b, [row_words("phi", n // GL, n % GL) for n in (2 * b, 2 * b + 1)], k, evac)

        def turn_rem(i, h, k, evac="S"):
            turn("rem%d_%d" % (i, h), [row_words("rem", i, g) for g in (2 * h, 2 * h + 1)], k, evac)

        def turn_force(c, rows, k, evac="S"):
            items = []
            for i in rows:
                words = t["force", i, c][:].bitcast(F32).rearrange("r (u p) -> r u p", u=2)
                items.append((("qforce", i, c), words))
            turn("force%d_%d" % (c, rows[0]), items, k, evac)

        def weave(g, c, eng):
            if ("woven", g, c) not in t:
                t["woven", g, c] = stage.tile([P, NT, 4], BF16, name="woven%d_%d" % (g, c), tag="woven", bufs=3, align_bytes=64)
            cut = WEAVE_V[c]
            cols = slice(cut, NT) if eng == "S" else slice(0, cut)
            dst = t["woven", g, c][:, cols, :].rearrange("p (a i) j -> p a j i", i=4)
            src = t["near_raw", g, c][:, :, cols].rearrange("p j (a i) -> p a j i", i=4)
            if eng == "S":
                nc.scalar.copy(out=dst, in_=src)
            else:
                nc.vector.tensor_copy(out=dst, in_=src)

        def quant_near(g, c):
            codes = keep.tile([P, NT], U32, name="near_codes%d_%d" % (g, c), align_bytes=64)
            plane = keep.tile([P, NT], U8, name="near_plane%d_%d" % (g, c), align_bytes=64)
            nc.vector.quantize_mx(
                out=codes[:].bitcast(FP8X4), scales=plane[:], in_=t["woven", g, c][:].rearrange("p n j -> p (n j)")
            )
            t["qnear", g, c] = (codes, plane)

        def sorted_phi(i, c):
            return t["phi", i][:, c * NT:(c + 1) * NT].rearrange("r (p u e) -> r u p e", u=2, e=2)

        def square(i, c):
            sq = stage.tile([P, 2, P, 2], F32, name="sq%d_%d" % (i, c), tag="sq", bufs=4)
            nc.scalar.activation(out=sq[:], in_=sorted_phi(i, c), func=ACT.Square)
            t["sq", i, c] = sq

        def couple(i, c):
            cub = keep.tile([P, 2, P, 2], F32, name="cubic%d_%d" % (i, c))
            lam_c = t["lam", c].rearrange("q u p -> q (u p)").bitcast(BF16).rearrange("q (u p e) -> q u p e", u=2, e=2)
            nc.vector.tensor_tensor(out=cub[:], in0=sorted_phi(i, c), in1=lam_c, op=ALU.mult)
            t["cubic", i, c] = cub

        def cube(i, c):
            cub = t["cubic", i, c]
            nc.vector.tensor_tensor(out=cub[:], in0=cub[:], in1=t["sq", i, c][:], op=ALU.mult)

        def open_group(i, c, k):
            t["lin", i, c] = bank(k, "lin%d_%d" % (i, c))
            t["passes", i, c] = 0

        def stage1_pass(i, c, lhs, rhs, rhs_scale):
            n = t["passes", i, c]
            nc.tensor.matmul_mx(
                out=t["lin", i, c][:], lhsT=lhs[0].bitcast(FP8X4), lhsT_scale=lhs[1], rhs=rhs, rhs_scale=rhs_scale,
                start=(n == 0), stop=(n == GL + GC - 1),
            )
            t["passes", i, c] = n + 1

        def near_pass(i, c, g):
            codes, plane = t["qnear", g, c]
            stage1_pass(i, c, t["qphi", i, g], codes[:].bitcast(FP8X4), plane[:])

        def far_pass(i, c, g):
            stage1_pass(i, c, t["qrem", i, g], t["far", c, g].bitcast(FP4X4), t["far_plane%d" % c][:, g, :])

        def far_passes(i, c):
            for g in range(GC):
                far_pass(i, c, g)

        def near_passes(i, c):
            for g in range(GL):
                near_pass(i, c, g)

        def force(i, c):
            f = stage.tile([P, NT], BF16, name="force%d_%d" % (i, c), tag="force", bufs=8)
            nc.vector.tensor_tensor(
                out=f[:].rearrange("r (u p e) -> r u p e", u=2, e=2),
                in0=t["lin", i, c][:].rearrange("r (p u e) -> r u p e", u=2, e=2),
                in1=t["cubic", i, c][:], op=ALU.subtract,
            )
            t["force", i, c] = f

        def kick_pass(i, m, g, k):
            if g == 0:
                t["kick", i, m] = bank(k, "kick%d_%d" % (i, m))
            codes, plane = t["qforce", i, g]
            nc.tensor.matmul_mx(
                out=t["kick", i, m][:], lhsT=codes.bitcast(FP8X4), lhsT_scale=plane,
                rhs=t["acc"][:, g, m * 2 * NT:(m + 1) * 2 * NT].bitcast(FP4X4),
                rhs_scale=t["acc_plane"][:, g, m * NT:(m + 1) * NT],
                start=(g == 0), stop=(g == GL - 1),
            )

        def kick(i, m, k):
            for g in range(GL):
                kick_pass(i, m, g, k)

        def kick_by_pass(i, ks, gs):
            for g in gs:
                for m in range(NC):
                    kick_pass(i, m, g, ks[m])

        def turn_phi_row(i, k0, k1):
            turn("phi%d_0" % i, [row_words("phi", i, 0), row_words("phi", i, 1)], k0, "S")
            turn("phi%d_1" % i, [row_words("phi", i, 2)], k1, "S")

        def finish(i, m, parts=1):
            width = NT // parts
            for j in range(parts):
                res = stage.tile([P, width], F32, name="res%d_%d_%d" % (i, m, j), tag="res", bufs=5)
                cols = slice(m * NT + j * width, m * NT + (j + 1) * width)
                nc.vector.tensor_tensor(out=res[:], in0=t["kick", i, m][:, j * width:(j + 1) * width], in1=t["mom", i][:, cols], op=ALU.add)
                nc.sync.dma_start(out=out[i * P:(i + 1) * P, cols], in_=res[:])

        def gather2(key):
            gather(key + "_0")
            gather(key + "_1")

        def quant2(key):
            quant_turned(key + "_0")
            quant_turned(key + "_1")

        def load_far_chunk(c):
            load_plane("far_plane%d" % c, far_scales, c, c + 1)
            load_far(c, 0, GC)


        load_lam()
        load_phi(0)
        load_remote(0)
        load_remote(1)
        t["ident"] = keep.tile([P, P], F32, name="ident")
        make_identity(nc, t["ident"][:])
        for c in range(NC):
            clear_plane("far_plane%d" % c, GC, NT, nc.vector)
        clear_plane("acc_plane", GL, L, nc.vector)
        load_plane("far_plane0", far_scales, 0, 1)
        load_far(0, 0, 2)
        load_far(0, 2, GC)
        for i in range(1, RT):
            load_near(i - 1, 0, 1)
            load_phi(i)
            if i + 1 < RT:
                load_remote(i + 1)
        for c in range(1, NC):
            load_near(0, c, c + 1)
            load_far_chunk(c)
            load_near(1, c, c + 1)
            load_near(2, c, c + 1)
        load_plane("acc_plane", acc_scales, 0, 3)
        load_acc()

        spread_lam(0, 1, 3)
        spread_lam(1, 3, 2)
        gather_lam(0)
        gather_lam(1)
        for c in range(NC):
            couple(0, c)
        square(0, 0)
        cube(0, 0)
        turn_phi_row(0, 4, 5)
        gather2("phi0")
        quant2("phi0")
        for i in range(2):
            turn_rem(i, 0, 6 - 2 * i)
            turn_rem(i, 1, 7 - 2 * i)
            gather2("rem%d" % i)
            quant2("rem%d" % i)
        for c in range(1, NC):
            square(0, c)
        cube(0, 1)
        for i in range(2):
            open_group(i, 0, i)
            far_pass(i, 0, 0)
            far_pass(i, 0, 1)
        far_pass(0, 0, 2)
        far_pass(0, 0, 3)
        done = []
        for i in range(1, RT):
            weave(i - 1, 0, "S")
            weave(i - 1, 0, "V")
            turn_phi_row(i, 6, 7)
            gather2("phi%d" % i)
            if i == 1:
                cube(0, 2)
            couple(i, 0)
            quant_near(i - 1, 0)
            quant2("phi%d" % i)
            if i > 1:
                open_group(i, 0, i)
            for g in range(2 if i == 1 else 0, GC):
                far_pass(i, 0, g)
            square(i, 0)
            if i + 1 < RT:
                turn_rem(i + 1, 0, 4)
                turn_rem(i + 1, 1, 5)
                gather2("rem%d" % (i + 1))
                if i == 1:
                    couple(i, 1)
                quant_turned("rem%d_0" % (i + 1))
                cube(i, 0)
                quant_turned("rem%d_1" % (i + 1))
            for r in range(i + 1):
                for g in range(i):
                    if (r, g) not in done:
                        near_pass(r, 0, g)
                        done.append((r, g))
        for i in range(RT):
            load_mom(i)

        for i in range(RT):
            open_group(i, 1, 4 + i)
            far_passes(i, 1)
        for g in range(GL):
            weave(g, 1, "S")
            weave(g, 1, "V")
            if g == 0:
                cube(RT - 1, 0)
            if g < 2:
                force(2 * g, 0)
                force(2 * g + 1, 0)
            else:
                couple(2, 1)
                couple(3, 1)
            quant_near(g, 1)
            square(g + 1, 1)
        turn_force(0, (0, 1), 0)
        turn_force(0, (2, 3), 1)
        for g in range(GL):
            for i in range(RT):
                near_pass(i, 1, g)
        for g in range(GL):
            weave(g, 2, "S")
            weave(g, 2, "V")
            cube(g + 1, 1)
            quant_near(g, 2)
        for i in range(2):
            open_group(i, 2, 2 + i)
            far_passes(i, 2)
        for i in range(2):
            near_passes(i, 2)
        gather("force0_0")
        square(1, 2)
        gather("force0_2")
        square(2, 2)
        square(3, 2)
        force(0, 1)
        force(1, 1)
        couple(1, 2)
        force(2, 1)
        force(3, 1)
        cube(1, 2)
        force(0, 2)
        force(1, 2)
        quant_turned("force0_0")
        open_group(2, 2, 0)
        far_passes(2, 2)
        near_passes(2, 2)
        open_group(3, 2, 1)
        far_passes(3, 2)
        turn_force(1, (0, 1), 4)
        turn_force(2, (0, 1), 5)
        turn_force(1, (2, 3), 6)
        near_passes(3, 2)
        couple(2, 2)
        quant_turned("force0_2")
        couple(3, 2)
        gather("force1_0")
        gather("force2_0")
        gather("force1_2")
        quant_turned("force1_0")
        cube(2, 2)
        quant_turned("force2_0")
        cube(3, 2)
        force(2, 2)
        force(3, 2)
        quant_turned("force1_2")
        kick_by_pass(0, (7, 2, 3), (0, 1, 2))
        for m in range(NC):
            finish(0, m)
        for m in range(2):
            kick(1, m, 4 + m)
            finish(1, m)
        turn_force(2, (2, 3), 0)
        gather("force2_2")
        quant_turned("force2_2")
        kick(1, 2, 6)
        finish(1, 2)
        for i in range(2, RT):
            for m in range(NC):
                kick(i, m, ((7, 2, 3), (1, 4, 5))[i - 2][m])
                finish(i, m, 2 if (i, m) == (RT - 1, NC - 1) else 1)
